import numpy as np
import ml_dtypes


def mxq(x, axis, fmt="e4m3"):
    dtype, down = {"e4m3": (ml_dtypes.float8_e4m3fn, 7), "e5m2": (ml_dtypes.float8_e5m2, 14)}[fmt]
    v = np.moveaxis(np.asarray(x, np.float32).astype(ml_dtypes.bfloat16).astype(np.float64), axis, -1)
    blocks = v.reshape(v.shape[:-1] + (-1, 32))
    amax = np.abs(blocks).max(-1, keepdims=True)
    byte = np.maximum(np.where(amax > 0, np.frexp(amax)[1] - 1 + 127, 0) - down, 1)
    scale = np.exp2(byte - 127.0)
    codes = (blocks / scale).astype(np.float32).astype(dtype).astype(np.float64)
    return np.moveaxis((codes * scale).reshape(v.shape), -1, axis)


WIDE = False


def mx_kscale(k):
    if not WIDE:
        return np.ones(k)
    levels = np.array([30, -30])
    if k % 512:
        return np.exp2(np.random.permutation(np.resize(levels, k // 32))).repeat(32)
    a = np.empty((k // 512, 16))
    for p in range(k // 512):
        a[p, :8] = np.random.permutation(np.resize(levels, 8))
        for g in range(8):
            far = levels[np.abs(levels - a[p, g]) >= 10]
            a[p, g + 8] = far[np.random.randint(len(far))]
    return np.exp2(a.ravel()).repeat(32)


def f64(x):
    return np.asarray(x).astype(np.float64)


def striped(idx):
    return np.tile(idx.reshape(-1, 16).T, (8, 1)).astype(np.uint16)


def unstriped(offs):
    return offs[:16].T.reshape(-1).astype(np.int64)


K, T, E, C, N = 256, 1024, 8, 512, 512
TOP = 4


def by_expert(wq, xq):
    return np.concatenate([wq[e].T @ xq[:, e * C:(e + 1) * C] for e in range(E)], axis=1)


def setup_inputs():
    n = np.random.standard_normal
    s = mx_kscale(N)[:, None]
    deal = np.repeat(np.arange(E), C).reshape(TOP, T)[:, np.random.permutation(T)]
    deal = np.take_along_axis(deal, np.argsort(np.random.rand(TOP, T), axis=0), axis=0)
    for _ in range(8):
        s_, t_ = np.random.permutation(T).reshape(2, -1); r = np.random.randint(TOP, size=T // 2); x, y = deal[r, s_].copy(), deal[r, t_].copy()
        ok = ~((deal[:, s_] == y).any(0) | (deal[:, t_] == x).any(0)); deal[r[ok], s_[ok]] = y[ok]; deal[r[ok], t_[ok]] = x[ok]
    order = np.lexsort((np.random.rand(TOP * T), deal.reshape(-1)))
    slot_token = order % T; pos = np.empty(TOP * T, np.int64); pos[order] = np.arange(TOP * T); pos = pos.reshape(TOP, T)
    g = np.random.uniform(0.5, 1.5, (TOP, T)); g = g / g.sum(0)
    w_slot = np.empty(E * C)
    for r in range(TOP): w_slot[pos[r]] = g[r]
    return {
        "dyT": (n((N, T)) * s).astype(np.float32),
        "w": (n((E + 1, N, K)) / np.sqrt(N) / s[None]).astype(np.float32),
        "gate": np.tile(w_slot, (N, 1)).astype(np.float32),
        "offs": striped(slot_token),
        "pos1": striped(pos[0]),
        "pos2": striped(pos[1]),
        "pos3": striped(pos[2]),
        "pos4": striped(pos[3]),
    }


def reference(dyT, w, gate, offs, pos1, pos2, pos3, pos4):
    idx = unstriped(offs)
    gq = mxq(f64(gate) * f64(dyT)[:, idx], 0, "e5m2")
    wq = mxq(f64(w), 1, "e4m3")
    ds = wq[E].T @ mxq(f64(dyT), 0, "e5m2")
    dx = by_expert(wq, gq)
    return ds + dx[:, unstriped(pos1)] + dx[:, unstriped(pos2)] + dx[:, unstriped(pos3)] + dx[:, unstriped(pos4)]

@@ -1,0 +1,263 @@
+from contextlib import ExitStack
+
+import concourse.mybir as mybir
+from concourse.masks import make_identity
+
+K, T, E, C, N = 256, 1024, 8, 512, 512
+TOP = 4
+FLOPS = 2 * N * K * (E * C + T)
+
+F32 = mybir.dt.float32
+BF16 = mybir.dt.bfloat16
+U32 = mybir.dt.uint32
+U16 = mybir.dt.uint16
+U8 = mybir.dt.uint8
+E4M3 = mybir.dt.float8_e4m3fn_x4
+E5M2 = mybir.dt.float8_e5m2_x4
+MULT = mybir.AluOpType.mult
+ADD = mybir.AluOpType.add
+
+P = 128
+PACK = 4
+STRIPE = 16
+BANK = 512
+HALVES = K // P
+RANGES = T // BANK
+LAST_PIECES = (256, 128, 128)
+
+
+def tile_moe_bds_lin_none_kernel(tc, dyT, w, gate, offs, pos1, pos2, pos3, pos4, out):
+    nc = tc.nc
+    with ExitStack() as ctx:
+        keep = ctx.enter_context(tc.tile_pool(name="keep", bufs=1))
+        ring = ctx.enter_context(tc.tile_pool(name="ring", bufs=2))
+        psum = ctx.enter_context(tc.psum_pool(name="psum", bufs=2))
+
+        dy_rows = dyT.rearrange("(p j) t -> p j t", j=PACK)
+        gate_rows = gate.rearrange("(p j) s -> p j s", j=PACK)
+
+        def interleave(dst, src):
+            nc.scalar.copy(
+                out=dst.rearrange("p (c i j) -> p c j i", i=4, j=PACK),
+                in_=src.rearrange("p j (c i) -> p c j i", i=4),
+            )
+
+        slot_token = keep.tile([P, E * C // STRIPE], U16, name="slot_token")
+        nc.sync.dma_start(slot_token[:], offs)
+
+        planes = [keep.tile([P, T], F32, name="plane%d" % j) for j in range(PACK)]
+        gates = {}
+        w_raw = {}
+
+        def new_gate(e):
+            gates[e] = ring.tile([P, PACK, C], F32, name="gate%d" % e, tag="quad", bufs=4)
+
+        def load_gate(e):
+            new_gate(e)
+            nc.sync.dma_start(gates[e][:], gate_rows[:, :, e * C : (e + 1) * C])
+
+        def load_w(e):
+            w_raw[e] = ring.tile([P, PACK, K], F32, name="w_raw%d" % e, tag="w_raw", bufs=4)
+            nc.sync.dma_start(w_raw[e][:], w[e].rearrange("(p j) k -> p j k", j=PACK))
+
+        new_gate(0)
+        new_gate(1)
+        for j in range(PACK):
+            nc.sync.dma_start(planes[j][:], dy_rows[:, j, :])
+            for e in range(2):
+                nc.sync.dma_start(gates[e][:, j, :], gate_rows[:, j, e * C : (e + 1) * C])
+
+        ident = keep.tile([P, P], F32, name="ident")
+        make_identity(nc, ident[:])
+
+        dx = [keep.tile([P, E * C], F32, name="dx%d" % h) for h in range(HALVES)]
+        ds = [keep.tile([P, T], F32, name="ds%d" % h) for h in range(HALVES)]
+        g_codes, g_scales, w_bf, w_codes, w_scales = {}, {}, {}, {}, {}
+
+        def gather_plane(dst, e, j, c0, n):
+            s0 = e * C + c0
+            nc.vector.tensor_tensor(
+                dst[:, j, :],
+                planes[j][:].indirect(slot_token[:, s0 // STRIPE : (s0 + n) // STRIPE]),
+                gates[e][:, j, c0 : c0 + n],
+                MULT,
+            )
+
+        def new_g(n):
+            return ring.tile([P, PACK, n], F32, name="g", tag="g", bufs=3)
+
+        def new_codes(e):
+            g_codes[e] = keep.tile([P, C], U32, name="g_codes%d" % e, align_bytes=64)
+            g_scales[e] = keep.tile([P, C], U8, name="g_scales%d" % e, align_bytes=64)
+
+        def quantize_g(g, e, c0, n):
+            g_bf = ring.tile([P, PACK * n], BF16, name="g_bf", tag="g_bf", bufs=3, align_bytes=64)
+            interleave(g_bf[:], g[:])
+            nc.vector.quantize_mx(
+                out=g_codes[e][:, c0 : c0 + n].bitcast(E5M2), scales=g_scales[e][:, c0 : c0 + n], in_=g_bf[:]
+            )
+
+        def interleave_w(e):
+            w_bf[e] = keep.tile([P, PACK * K], BF16, name="w_bf%d" % e, align_bytes=64)
+            interleave(w_bf[e][:], w_raw[e][:])
+
+        def quantize_w(e, h):
+            w_codes[e, h] = keep.tile([P, P], U32, name="w_codes%d_%d" % (e, h), align_bytes=64)
+            w_scales[e, h] = keep.tile([P, P], U8, name="w_scales%d_%d" % (e, h), align_bytes=64)
+            nc.vector.quantize_mx(
+                out=w_codes[e, h][:].bitcast(E4M3),
+                scales=w_scales[e, h][:],
+                in_=w_bf[e][:, h * PACK * P : (h + 1) * PACK * P],
+            )
+
+        def product(dst, e, h, codes, scales):
+            sums = psum.tile([P, BANK], F32, name="sums", tag="sums%d" % h)
+            nc.tensor.matmul_mx(
+                out=sums[:],
+                lhsT=w_codes[e, h][:].bitcast(E4M3),
+                lhsT_scale=w_scales[e, h][:],
+                rhs=codes.bitcast(E5M2),
+                rhs_scale=scales,
+                start=True,
+                stop=True,
+            )
+            nc.scalar.copy(out=dst, in_=sums[:])
+
+        def expert_half(e, h):
+            product(dx[h][:, e * C : (e + 1) * C], e, h, g_codes[e][:], g_scales[e][:])
+
+        def finish_expert(e, g):
+            new_codes(e)
+            interleave_w(e)
+            quantize_g(g, e, 0, C)
+            quantize_w(e, 0)
+            expert_half(e, 0)
+
+        dy_all = keep.tile([P, PACK, T], F32, name="dy_all")
+        token_slots = [keep.tile([P, T // STRIPE], U16, name="token_slots%d" % r) for r in range(TOP)]
+
+        load_gate(2)
+        load_w(0)
+        load_gate(3)
+        load_w(1)
+        load_w(2)
+        load_w(3)
+        g_first = [new_g(C) for e in range(2)]
+        for j in range(PACK):
+            for e in range(2):
+                gather_plane(g_first[e], e, j, 0, C)
+        pending = [(0, g_first[0]), (1, g_first[1])]
+
+        for e in range(2, E - 1):
+            if e + 2 < E:
+                load_gate(e + 2)
+            if e == 2:
+                nc.sync.dma_start(dy_all[:], dy_rows)
+            g = new_g(C)
+            for j in range(PACK):
+                gather_plane(g, e, j, 0, C)
+                if j % 2 == 1 and pending:
+                    finish_expert(*pending.pop(0))
+            pending.append((e, g))
+            if e + 2 < E:
+                load_w(e + 2)
+            if e == 3:
+                for r, pos in enumerate((pos1, pos2, pos3, pos4)):
+                    nc.sync.dma_start(token_slots[r][:], pos)
+            if e == 4:
+                load_w(E)
+
+        e = E - 1
+        new_codes(e)
+        c0 = 0
+        waiting = None
+        for n in LAST_PIECES:
+            g = new_g(n)
+            for j in range(PACK):
+                gather_plane(g, e, j, c0, n)
+                if j == 1 and pending:
+                    finish_expert(*pending.pop(0))
+                    interleave_w(e)
+                    quantize_w(e, 0)
+            if waiting is not None:
+                quantize_g(*waiting)
+            waiting = (g, e, c0, n)
+            c0 += n
+        quantize_g(*waiting)
+        expert_half(e, 0)
+
+        interleave_w(E)
+        dy_codes, dy_scales = {}, {}
+        for r in range(RANGES):
+            dy_bf = keep.tile([P, PACK * BANK], BF16, name="dy_bf%d" % r, align_bytes=64)
+            interleave(dy_bf[:], dy_all[:, :, r * BANK : (r + 1) * BANK])
+            dy_codes[r] = keep.tile([P, BANK], U32, name="dy_codes%d" % r, align_bytes=64)
+            dy_scales[r] = keep.tile([P, BANK], U8, name="dy_scales%d" % r, align_bytes=64)
+            nc.vector.quantize_mx(out=dy_codes[r][:].bitcast(E5M2), scales=dy_scales[r][:], in_=dy_bf[:])
+        for h in range(HALVES):
+            quantize_w(E, h)
+        for e in range(E):
+            quantize_w(e, 1)
+
+        def shared_half(h):
+            for r in range(RANGES):
+                product(ds[h][:, r * BANK : (r + 1) * BANK], E, h, dy_codes[r][:], dy_scales[r][:])
+
+        shared_half(0)
+        for e in range(E):
+            expert_half(e, 1)
+        shared_half(1)
+
+        def fetch(dst, h, r, i):
+            cols = BANK // STRIPE
+            nc.vector.tensor_copy(dst[:, i, :], dx[h][:].indirect(token_slots[i][:, r * cols : (r + 1) * cols]))
+
+        def turn(dst, src, first, last):
+            blocks = BANK // P
+            for b in range(blocks):
+                nc.tensor.matmul(
+                    dst[:, b * P : (b + 1) * P],
+                    src[:, b * P : (b + 1) * P],
+                    ident[:],
+                    start=(first and b == 0),
+                    stop=(last and b == blocks - 1),
+                    is_transpose=True,
+                )
+
+        def summed(h, r, fetched, terms):
+            turned = psum.tile([P, BANK], F32, name="turned")
+            turn(turned, ds[h][:, r * BANK : (r + 1) * BANK], True, False)
+            for i in range(terms):
+                turn(turned, fetched[:, i, :], False, i == terms - 1)
+            turned_sb = ring.tile([P, BANK], F32, name="turned_sb")
+            nc.scalar.copy(out=turned_sb[:], in_=turned[:])
+            back = psum.tile([P, BANK], F32, name="back")
+            for b in range(BANK // P):
+                nc.tensor.transpose(back[:, b * P : (b + 1) * P], turned_sb[:, b * P : (b + 1) * P], ident[:])
+            return back
+
+        def store(h, r, result):
+            nc.sync.dma_start(out[h * P : (h + 1) * P, r * BANK : (r + 1) * BANK], result[:])
+
+        for r in range(RANGES):
+            fetched = ring.tile([P, TOP, BANK], F32, name="fetched", tag="quad", bufs=4)
+            for i in range(TOP):
+                fetch(fetched, 0, r, i)
+            back = summed(0, r, fetched, TOP)
+            result = ring.tile([P, BANK], F32, name="result", bufs=4)
+            nc.scalar.copy(out=result[:], in_=back[:])
+            store(0, r, result)
+
+        tail = []
+        for r in range(RANGES):
+            fetched = ring.tile([P, TOP, BANK], F32, name="fetched", tag="quad", bufs=4)
+            for i in range(TOP - 1):
+                fetch(fetched, 1, r, i)
+            tail.append((fetched, summed(1, r, fetched, TOP - 1)))
+        for r in range(RANGES):
+            fetch(tail[r][0], 1, r, TOP - 1)
+        for r in range(RANGES):
+            fetched, back = tail[r]
+            result = ring.tile([P, BANK], F32, name="result", bufs=4)
+            nc.vector.tensor_tensor(result[:], fetched[:, TOP - 1, :], back[:], ADD)
+            store(1, r, result)

@@ -24,6 +24,13 @@ BANK = 512
 HALVES = K // P
 RANGES = T // BANK
 LAST_PIECES = (256, 128, 128)
+DY_CUTS = (0, 384, 512, 1024)
+GATE_LAST = True
+GATE_BYTES = 4 * PACK * C
+W_HOME = (3, 3, 3, 4, 5, 6, 7, 7, 7)
+TB = 2
+LOADS = "p2 w0 w1 g3 w2 w3 g4 w4 w5 g5 w6 d0 g6 w7 w8 g7 l0 d1"
+ORDER = "G2 I0 I1 G3 A0 A1 I2 A2 B0 B1 B2 G4 I3 A3 E0 E1 E2 B3 G5 I4 A4 E3 B4 D0 G6 I5 A5 E4 B5 G7 A6 A7 I6 E5 I7 W8 B6 D1 B7 E6 E7 Q0 H0 S0 D2 Q1 F0 F1 F2 F3 F4 S1 F5 F6 F7 S2 S3"
 
 
 def tile_moe_bds_lin_none_kernel(tc, dyT, w, gate, offs, pos1, pos2, pos3, pos4, out):
@@ -31,6 +38,7 @@ def tile_moe_bds_lin_none_kernel(tc, dyT, w, gate, offs, pos1, pos2, pos3, pos4,
     with ExitStack() as ctx:
         keep = ctx.enter_context(tc.tile_pool(name="keep", bufs=1))
         ring = ctx.enter_context(tc.tile_pool(name="ring", bufs=2))
+        arena = ctx.enter_context(tc.tile_pool(name="arena", bufs=1))
         psum = ctx.enter_context(tc.psum_pool(name="psum", bufs=2))
 
         dy_rows = dyT.rearrange("(p j) t -> p j t", j=PACK)
@@ -50,14 +58,23 @@ def tile_moe_bds_lin_none_kernel(tc, dyT, w, gate, offs, pos1, pos2, pos3, pos4,
         w_raw = {}
 
         def new_gate(e):
-            gates[e] = ring.tile([P, PACK, C], F32, name="gate%d" % e, tag="quad", bufs=4)
+            head = arena.tile([P, PACK - 1, C], F32, name="gate%d" % e, offset=e * GATE_BYTES, align_bytes=64)
+            last = arena.tile([P, C], F32, name="gate_last%d" % e, offset=(e + 1) * GATE_BYTES - 4 * C, align_bytes=64)
+            gates[e] = [head[:, j, :] for j in range(PACK - 1)] + [last[:]]
+            return head
 
         def load_gate(e):
+            head = new_gate(e)
+            nc.sync.dma_start(head[:], gate_rows[:, 0 : PACK - 1, e * C : (e + 1) * C])
+            nc.sync.dma_start(gates[e][PACK - 1], gate_rows[:, PACK - 1, e * C : (e + 1) * C])
+
+        def load_gate_planes(e):
             new_gate(e)
-            nc.sync.dma_start(gates[e][:], gate_rows[:, :, e * C : (e + 1) * C])
+            for j in range(PACK):
+                nc.sync.dma_start(gates[e][j], gate_rows[:, j, e * C : (e + 1) * C])
 
         def load_w(e):
-            w_raw[e] = ring.tile([P, PACK, K], F32, name="w_raw%d" % e, tag="w_raw", bufs=4)
+            w_raw[e] = ring.tile([P, PACK, K], F32, name="w_raw%d" % e, tag="w_raw", bufs=E)
             nc.sync.dma_start(w_raw[e][:], w[e].rearrange("(p j) k -> p j k", j=PACK))
 
         new_gate(0)
@@ -65,152 +82,185 @@ def tile_moe_bds_lin_none_kernel(tc, dyT, w, gate, offs, pos1, pos2, pos3, pos4,
         for j in range(PACK):
             nc.sync.dma_start(planes[j][:], dy_rows[:, j, :])
             for e in range(2):
-                nc.sync.dma_start(gates[e][:, j, :], gate_rows[:, j, e * C : (e + 1) * C])
+                nc.sync.dma_start(gates[e][j], gate_rows[:, j, e * C : (e + 1) * C])
 
         ident = keep.tile([P, P], F32, name="ident")
         make_identity(nc, ident[:])
 
         dx = [keep.tile([P, E * C], F32, name="dx%d" % h) for h in range(HALVES)]
-        ds = [keep.tile([P, T], F32, name="ds%d" % h) for h in range(HALVES)]
-        g_codes, g_scales, w_bf, w_codes, w_scales = {}, {}, {}, {}, {}
+        g_codes, g_scales = {}, {}
+        used = {e: 0 for e in range(E + 1)}
 
-        def gather_plane(dst, e, j, c0, n):
+        def after_gate(e, shape, dtype, size, name):
+            start = e * GATE_BYTES + used[e]
+            used[e] += size
+            assert used[e] <= GATE_BYTES
+            return arena.tile(shape, dtype, name=name, offset=start, align_bytes=64)
+
+        w_codes, w_scales = {}, {}
+        late_codes = keep.tile([P, E * P], U32, name="late_codes", align_bytes=64)
+        late_scales = keep.tile([P, E * P], U8, name="late_scales", align_bytes=64)
+        late_stage = keep.tile([P, TOP * BANK], F32, name="late_stage", align_bytes=64)
+        late_bf = late_stage[:].bitcast(BF16)
+        dy_codes = [keep.tile([P, BANK], U32, name="dy_codes%d" % r, align_bytes=64) for r in range(RANGES)]
+        dy_scales = [keep.tile([P, BANK], U8, name="dy_scales%d" % r, align_bytes=64) for r in range(RANGES)]
+        dy_raw = [keep.tile([P, PACK * BANK], F32, name="dy_raw%d" % r) for r in range(RANGES)]
+        dy_planes = [raw[:].rearrange("p (j t) -> p j t", j=PACK) for raw in dy_raw]
+        first_stage = keep.tile([P, 2 * BANK], F32, name="first_stage", align_bytes=64)
+        first_bf = first_stage[:].bitcast(BF16)
+        dy_bf = [first_bf, late_bf[:, 0 : PACK * BANK]]
+        token_slots = [keep.tile([P, T // STRIPE], U16, name="token_slots%d" % r) for r in range(TOP)]
+        banks = [psum.tile([P, BANK], F32, name="bank%d" % b, bufs=1) for b in range(4)]
+        turned_banks = [psum.tile([P, BANK], F32, name="turned%d" % b, bufs=1) for b in range(TB)]
+        back_banks = [psum.tile([P, BANK], F32, name="back%d" % b, bufs=1) for b in range(TB)]
+        ds = {}
+        g = {0: keep.tile([P, PACK * C], F32, name="g_first")}
+
+        def load_dy(r):
+            nc.sync.dma_start(dy_planes[r], dy_rows[:, :, r * BANK : (r + 1) * BANK])
+
+        def load_lists(i):
+            for r, pos in enumerate((pos1, pos2, pos3, pos4)):
+                nc.sync.dma_start(token_slots[r][:], pos)
+
+        def piece(e, c0, n):
+            return g[e][:, PACK * c0 : PACK * (c0 + n)].rearrange("p (j c) -> p j c", j=PACK)
+
+        def gather_plane(e, j, c0, n):
             s0 = e * C + c0
             nc.vector.tensor_tensor(
-                dst[:, j, :],
+                piece(e, c0, n)[:, j, :],
                 planes[j][:].indirect(slot_token[:, s0 // STRIPE : (s0 + n) // STRIPE]),
-                gates[e][:, j, c0 : c0 + n],
+                gates[e][j][:, c0 : c0 + n],
                 MULT,
             )
 
-        def new_g(n):
-            return ring.tile([P, PACK, n], F32, name="g", tag="g", bufs=3)
+        def pieces(e):
+            sizes = LAST_PIECES if e == E - 1 else (C,)
+            return [(sum(sizes[:i]), n) for i, n in enumerate(sizes)]
 
-        def new_codes(e):
-            g_codes[e] = keep.tile([P, C], U32, name="g_codes%d" % e, align_bytes=64)
-            g_scales[e] = keep.tile([P, C], U8, name="g_scales%d" % e, align_bytes=64)
+        def gather_expert(e):
+            g[e] = ring.tile([P, PACK * C], F32, name="g")
+            for c0, n in pieces(e):
+                for j in range(PACK):
+                    gather_plane(e, j, c0, n)
 
-        def quantize_g(g, e, c0, n):
-            g_bf = ring.tile([P, PACK * n], BF16, name="g_bf", tag="g_bf", bufs=3, align_bytes=64)
-            interleave(g_bf[:], g[:])
+        def quantize_g(e):
+            home = max(e + 1, 2)
+            g_codes[e] = after_gate(home, [P, C], U32, 4 * C, "g_codes%d" % e)
+            g_scales[e] = after_gate(home, [P, C], U8, C, "g_scales%d" % e)
+            for c0, n in pieces(e):
+                if GATE_LAST and e == E - 1 and c0 + n == C:
+                    g_bf = late_bf[:, PACK * P * (E - 1) : PACK * P * E]
+                elif GATE_LAST and e == E - 1 and c0 + 2 * n == C and c0 > 0:
+                    g_bf = first_bf[:, PACK * (BANK - n) : PACK * BANK]
+                else:
+                    g_bf = ring.tile([P, PACK * n], BF16, name="g_bf", bufs=3, align_bytes=64)
+                interleave(g_bf[:], piece(e, c0, n))
+                nc.vector.quantize_mx(
+                    out=g_codes[e][:, c0 : c0 + n].bitcast(E5M2), scales=g_scales[e][:, c0 : c0 + n], in_=g_bf[:]
+                )
+
+        def quantize_w(e, halves):
+            n = halves * P
+            w_bf = ring.tile([P, PACK * n], BF16, name="w_bf", bufs=4, align_bytes=64)
+            interleave(w_bf[:], w_raw[e][:, :, 0:n])
+            home = W_HOME[e]
+            codes = after_gate(home, [P, n], U32, 4 * n, "w_codes%d" % e)
+            scales = after_gate(home, [P, n], U8, n, "w_scales%d" % e)
+            nc.vector.quantize_mx(out=codes[:].bitcast(E4M3), scales=scales[:], in_=w_bf[:])
+            for h in range(halves):
+                w_codes[e, h] = codes[:, h * P : (h + 1) * P]
+                w_scales[e, h] = scales[:, h * P : (h + 1) * P]
+
+        def interleave_late(e):
+            interleave(late_bf[:, PACK * P * e : PACK * P * (e + 1)], w_raw[e][:, :, P:K])
+
+        def quantize_late(i):
+            nc.vector.quantize_mx(out=late_codes[:].bitcast(E4M3), scales=late_scales[:], in_=late_bf)
+            for e in range(E):
+                w_codes[e, 1] = late_codes[:, e * P : (e + 1) * P]
+                w_scales[e, 1] = late_scales[:, e * P : (e + 1) * P]
+
+        def interleave_dy(i):
+            t0, t1 = DY_CUTS[i], DY_CUTS[i + 1]
+            r = t0 // BANK
+            interleave(dy_bf[r][:, PACK * (t0 - r * BANK) : PACK * (t1 - r * BANK)], dy_planes[r][:, :, t0 - r * BANK : t1 - r * BANK])
+
+        def quantize_dy(r):
             nc.vector.quantize_mx(
-                out=g_codes[e][:, c0 : c0 + n].bitcast(E5M2), scales=g_scales[e][:, c0 : c0 + n], in_=g_bf[:]
+                out=dy_codes[r][:].bitcast(E5M2),
+                scales=dy_scales[r][:],
+                in_=dy_bf[r],
             )
 
-        def interleave_w(e):
-            w_bf[e] = keep.tile([P, PACK * K], BF16, name="w_bf%d" % e, align_bytes=64)
-            interleave(w_bf[e][:], w_raw[e][:])
-
-        def quantize_w(e, h):
-            w_codes[e, h] = keep.tile([P, P], U32, name="w_codes%d_%d" % (e, h), align_bytes=64)
-            w_scales[e, h] = keep.tile([P, P], U8, name="w_scales%d_%d" % (e, h), align_bytes=64)
-            nc.vector.quantize_mx(
-                out=w_codes[e, h][:].bitcast(E4M3),
-                scales=w_scales[e, h][:],
-                in_=w_bf[e][:, h * PACK * P : (h + 1) * PACK * P],
-            )
-
-        def product(dst, e, h, codes, scales):
-            sums = psum.tile([P, BANK], F32, name="sums", tag="sums%d" % h)
+        def product(dst, sums, e, h, codes, scales):
             nc.tensor.matmul_mx(
                 out=sums[:],
-                lhsT=w_codes[e, h][:].bitcast(E4M3),
-                lhsT_scale=w_scales[e, h][:],
-                rhs=codes.bitcast(E5M2),
-                rhs_scale=scales,
+                lhsT=w_codes[e, h].bitcast(E4M3),
+                lhsT_scale=w_scales[e, h],
+                rhs=codes[:].bitcast(E5M2),
+                rhs_scale=scales[:],
                 start=True,
                 stop=True,
             )
             nc.scalar.copy(out=dst, in_=sums[:])
 
-        def expert_half(e, h):
-            product(dx[h][:, e * C : (e + 1) * C], e, h, g_codes[e][:], g_scales[e][:])
+        second_banks = turned_banks + back_banks + [banks[3], banks[2], banks[0], banks[1]]
+        shared_banks = [banks[3], banks[3], banks[2], banks[0]]
 
-        def finish_expert(e, g):
-            new_codes(e)
-            interleave_w(e)
-            quantize_g(g, e, 0, C)
-            quantize_w(e, 0)
-            expert_half(e, 0)
+        def first_half(e):
+            product(dx[0][:, e * C : (e + 1) * C], banks[e % 3], e, 0, g_codes[e], g_scales[e])
 
-        dy_all = keep.tile([P, PACK, T], F32, name="dy_all")
-        token_slots = [keep.tile([P, T // STRIPE], U16, name="token_slots%d" % r) for r in range(TOP)]
+        def second_half(e):
+            product(dx[1][:, e * C : (e + 1) * C], second_banks[e], e, 1, g_codes[e], g_scales[e])
 
-        load_gate(2)
-        load_w(0)
-        load_gate(3)
-        load_w(1)
-        load_w(2)
-        load_w(3)
-        g_first = [new_g(C) for e in range(2)]
+        def shared(i):
+            h, r = divmod(i, RANGES)
+            ds[h, r] = ring.tile([P, BANK], F32, name="ds", tag="w_raw", bufs=E)
+            product(ds[h, r][:], shared_banks[i], E, h, dy_codes[r], dy_scales[r])
+
+        steps = {
+            "g": load_gate,
+            "p": load_gate_planes,
+            "w": load_w,
+            "d": load_dy,
+            "l": load_lists,
+            "G": gather_expert,
+            "I": quantize_g,
+            "W": lambda e: quantize_w(e, HALVES),
+            "A": lambda e: quantize_w(e, 1),
+            "B": interleave_late,
+            "H": quantize_late,
+            "D": interleave_dy,
+            "Q": quantize_dy,
+            "E": first_half,
+            "F": second_half,
+            "S": shared,
+        }
+        for step in LOADS.split():
+            steps[step[0]](int(step[1]))
+        g[1] = ring.tile([P, PACK * C], F32, name="g")
         for j in range(PACK):
             for e in range(2):
-                gather_plane(g_first[e], e, j, 0, C)
-        pending = [(0, g_first[0]), (1, g_first[1])]
+                gather_plane(e, j, 0, C)
+        for step in ORDER.split():
+            steps[step[0]](int(step[1]))
 
-        for e in range(2, E - 1):
-            if e + 2 < E:
-                load_gate(e + 2)
-            if e == 2:
-                nc.sync.dma_start(dy_all[:], dy_rows)
-            g = new_g(C)
-            for j in range(PACK):
-                gather_plane(g, e, j, 0, C)
-                if j % 2 == 1 and pending:
-                    finish_expert(*pending.pop(0))
-            pending.append((e, g))
-            if e + 2 < E:
-                load_w(e + 2)
-            if e == 3:
-                for r, pos in enumerate((pos1, pos2, pos3, pos4)):
-                    nc.sync.dma_start(token_slots[r][:], pos)
-            if e == 4:
-                load_w(E)
+        def quarters(tile, first, count):
+            return [tile[:, q * BANK : (q + 1) * BANK] for q in range(first, first + count)]
 
-        e = E - 1
-        new_codes(e)
-        c0 = 0
-        waiting = None
-        for n in LAST_PIECES:
-            g = new_g(n)
-            for j in range(PACK):
-                gather_plane(g, e, j, c0, n)
-                if j == 1 and pending:
-                    finish_expert(*pending.pop(0))
-                    interleave_w(e)
-                    quantize_w(e, 0)
-            if waiting is not None:
-                quantize_g(*waiting)
-            waiting = (g, e, c0, n)
-            c0 += n
-        quantize_g(*waiting)
-        expert_half(e, 0)
-
-        interleave_w(E)
-        dy_codes, dy_scales = {}, {}
-        for r in range(RANGES):
-            dy_bf = keep.tile([P, PACK * BANK], BF16, name="dy_bf%d" % r, align_bytes=64)
-            interleave(dy_bf[:], dy_all[:, :, r * BANK : (r + 1) * BANK])
-            dy_codes[r] = keep.tile([P, BANK], U32, name="dy_codes%d" % r, align_bytes=64)
-            dy_scales[r] = keep.tile([P, BANK], U8, name="dy_scales%d" % r, align_bytes=64)
-            nc.vector.quantize_mx(out=dy_codes[r][:].bitcast(E5M2), scales=dy_scales[r][:], in_=dy_bf[:])
-        for h in range(HALVES):
-            quantize_w(E, h)
-        for e in range(E):
-            quantize_w(e, 1)
-
-        def shared_half(h):
-            for r in range(RANGES):
-                product(ds[h][:, r * BANK : (r + 1) * BANK], E, h, dy_codes[r][:], dy_scales[r][:])
-
-        shared_half(0)
-        for e in range(E):
-            expert_half(e, 1)
-        shared_half(1)
+        spare = [after_gate(e, [P, TOP * BANK], F32, GATE_BYTES, "spare%d" % e) for e in range(2)]
+        fetch_rooms = [
+            quarters(late_stage, 2, 2) + quarters(first_stage, 0, 2),
+            quarters(late_stage, 0, 2) + quarters(dy_raw[1], 0, 2),
+            quarters(spare[0], 0, TOP),
+            quarters(spare[1], 0, TOP),
+        ]
 
         def fetch(dst, h, r, i):
             cols = BANK // STRIPE
-            nc.vector.tensor_copy(dst[:, i, :], dx[h][:].indirect(token_slots[i][:, r * cols : (r + 1) * cols]))
+            nc.vector.tensor_copy(dst[i], dx[h][:].indirect(token_slots[i][:, r * cols : (r + 1) * cols]))
 
         def turn(dst, src, first, last):
             blocks = BANK // P
@@ -225,13 +275,13 @@ def tile_moe_bds_lin_none_kernel(tc, dyT, w, gate, offs, pos1, pos2, pos3, pos4,
                 )
 
         def summed(h, r, fetched, terms):
-            turned = psum.tile([P, BANK], F32, name="turned")
-            turn(turned, ds[h][:, r * BANK : (r + 1) * BANK], True, False)
+            turned = turned_banks[(h * RANGES + r) % TB]
+            turn(turned, ds[h, r], True, False)
             for i in range(terms):
-                turn(turned, fetched[:, i, :], False, i == terms - 1)
-            turned_sb = ring.tile([P, BANK], F32, name="turned_sb")
+                turn(turned, fetched[i], False, i == terms - 1)
+            turned_sb = ring.tile([P, BANK], F32, name="turned_sb", tag="w_raw", bufs=E)
             nc.scalar.copy(out=turned_sb[:], in_=turned[:])
-            back = psum.tile([P, BANK], F32, name="back")
+            back = back_banks[(h * RANGES + r) % TB]
             for b in range(BANK // P):
                 nc.tensor.transpose(back[:, b * P : (b + 1) * P], turned_sb[:, b * P : (b + 1) * P], ident[:])
             return back
@@ -240,17 +290,17 @@ def tile_moe_bds_lin_none_kernel(tc, dyT, w, gate, offs, pos1, pos2, pos3, pos4,
             nc.sync.dma_start(out[h * P : (h + 1) * P, r * BANK : (r + 1) * BANK], result[:])
 
         for r in range(RANGES):
-            fetched = ring.tile([P, TOP, BANK], F32, name="fetched", tag="quad", bufs=4)
+            fetched = fetch_rooms[r]
             for i in range(TOP):
                 fetch(fetched, 0, r, i)
             back = summed(0, r, fetched, TOP)
-            result = ring.tile([P, BANK], F32, name="result", bufs=4)
+            result = ring.tile([P, BANK], F32, name="result", tag="w_raw", bufs=E)
             nc.scalar.copy(out=result[:], in_=back[:])
             store(0, r, result)
 
         tail = []
         for r in range(RANGES):
-            fetched = ring.tile([P, TOP, BANK], F32, name="fetched", tag="quad", bufs=4)
+            fetched = fetch_rooms[RANGES + r]
             for i in range(TOP - 1):
                 fetch(fetched, 1, r, i)
             tail.append((fetched, summed(1, r, fetched, TOP - 1)))
@@ -258,6 +308,6 @@ def tile_moe_bds_lin_none_kernel(tc, dyT, w, gate, offs, pos1, pos2, pos3, pos4,
             fetch(tail[r][0], 1, r, TOP - 1)
         for r in range(RANGES):
             fetched, back = tail[r]
-            result = ring.tile([P, BANK], F32, name="result", bufs=4)
-            nc.vector.tensor_tensor(result[:], fetched[:, TOP - 1, :], back[:], ADD)
+            result = ring.tile([P, BANK], F32, name="result", tag="w_raw", bufs=E)
+            nc.vector.tensor_tensor(result[:], fetched[TOP - 1], back[:], ADD)
             store(1, r, result)

@@ -24,13 +24,12 @@ BANK = 512
 HALVES = K // P
 RANGES = T // BANK
 LAST_PIECES = (256, 128, 128)
-DY_CUTS = (0, 384, 512, 1024)
-GATE_LAST = True
 GATE_BYTES = 4 * PACK * C
+LAST_STAGE = E * GATE_BYTES + 4096
 W_HOME = (3, 3, 3, 4, 5, 6, 7, 7, 7)
 TB = 2
-LOADS = "p2 w0 w1 g3 w2 w3 g4 w4 w5 g5 w6 d0 g6 w7 w8 g7 l0 d1"
-ORDER = "G2 I0 I1 G3 A0 A1 I2 A2 B0 B1 B2 G4 I3 A3 E0 E1 E2 B3 G5 I4 A4 E3 B4 D0 G6 I5 A5 E4 B5 G7 A6 A7 I6 E5 I7 W8 B6 D1 B7 E6 E7 Q0 H0 S0 D2 Q1 F0 F1 F2 F3 F4 S1 F5 F6 F7 S2 S3"
+LOADS = "p2 w0 w1 g3 w2 w3 w4 g4 w8 w5 g5 d0 w6 g6 w7 g7 l0 d1"
+ORDER = "G2 I0 I1 G3 A0 A1 I2 A2 G4 I3 A3 E0 E1 E2 G5 I4 A4 E3 G6 I5 A5 E4 G7 I6 A6 A7 D0 B0 B1 B2 B3 B4 B5 B6 B7 I7 E5 E6 E7 Q0 W8 H0 D1 Q1 F0 F1 F2 F3 F4 F5 F6 F7 S0 S1 S2 S3"
 
 
 def tile_moe_bds_lin_none_kernel(tc, dyT, w, gate, offs, pos1, pos2, pos3, pos4, out):
@@ -46,8 +45,8 @@ def tile_moe_bds_lin_none_kernel(tc, dyT, w, gate, offs, pos1, pos2, pos3, pos4,
 
         def interleave(dst, src):
             nc.scalar.copy(
-                out=dst.rearrange("p (c i j) -> p c j i", i=4, j=PACK),
-                in_=src.rearrange("p j (c i) -> p c j i", i=4),
+                dst.rearrange("p (c i j) -> p c j i", i=4, j=PACK),
+                src.rearrange("p j (c i) -> p c j i", i=4),
             )
 
         slot_token = keep.tile([P, E * C // STRIPE], U16, name="slot_token")
@@ -99,16 +98,14 @@ def tile_moe_bds_lin_none_kernel(tc, dyT, w, gate, offs, pos1, pos2, pos3, pos4,
 
         w_codes, w_scales = {}, {}
         late_codes = keep.tile([P, E * P], U32, name="late_codes", align_bytes=64)
-        late_scales = keep.tile([P, E * P], U8, name="late_scales", align_bytes=64)
         late_stage = keep.tile([P, TOP * BANK], F32, name="late_stage", align_bytes=64)
         late_bf = late_stage[:].bitcast(BF16)
         dy_codes = [keep.tile([P, BANK], U32, name="dy_codes%d" % r, align_bytes=64) for r in range(RANGES)]
-        dy_scales = [keep.tile([P, BANK], U8, name="dy_scales%d" % r, align_bytes=64) for r in range(RANGES)]
+        dy_scales = {}
         dy_raw = [keep.tile([P, PACK * BANK], F32, name="dy_raw%d" % r) for r in range(RANGES)]
         dy_planes = [raw[:].rearrange("p (j t) -> p j t", j=PACK) for raw in dy_raw]
-        first_stage = keep.tile([P, 2 * BANK], F32, name="first_stage", align_bytes=64)
-        first_bf = first_stage[:].bitcast(BF16)
-        dy_bf = [first_bf, late_bf[:, 0 : PACK * BANK]]
+        first_stage = keep.tile([P, T], F32, name="first_stage", align_bytes=64)
+        dy_bf = [first_stage[:].bitcast(BF16), late_bf[:, 0 : PACK * BANK]]
         token_slots = [keep.tile([P, T // STRIPE], U16, name="token_slots%d" % r) for r in range(TOP)]
         banks = [psum.tile([P, BANK], F32, name="bank%d" % b, bufs=1) for b in range(4)]
         turned_banks = [psum.tile([P, BANK], F32, name="turned%d" % b, bufs=1) for b in range(TB)]
@@ -150,10 +147,8 @@ def tile_moe_bds_lin_none_kernel(tc, dyT, w, gate, offs, pos1, pos2, pos3, pos4,
             g_codes[e] = after_gate(home, [P, C], U32, 4 * C, "g_codes%d" % e)
             g_scales[e] = after_gate(home, [P, C], U8, C, "g_scales%d" % e)
             for c0, n in pieces(e):
-                if GATE_LAST and e == E - 1 and c0 + n == C:
-                    g_bf = late_bf[:, PACK * P * (E - 1) : PACK * P * E]
-                elif GATE_LAST and e == E - 1 and c0 + 2 * n == C and c0 > 0:
-                    g_bf = first_bf[:, PACK * (BANK - n) : PACK * BANK]
+                if e == E - 1 and c0 + n == C:
+                    g_bf = arena.tile([P, PACK * n], BF16, name="last_bf", offset=LAST_STAGE, align_bytes=64)
                 else:
                     g_bf = ring.tile([P, PACK * n], BF16, name="g_bf", bufs=3, align_bytes=64)
                 interleave(g_bf[:], piece(e, c0, n))
@@ -163,7 +158,7 @@ def tile_moe_bds_lin_none_kernel(tc, dyT, w, gate, offs, pos1, pos2, pos3, pos4,
 
         def quantize_w(e, halves):
             n = halves * P
-            w_bf = ring.tile([P, PACK * n], BF16, name="w_bf", bufs=4, align_bytes=64)
+            w_bf = ring.tile([P, PACK * n], BF16, name="w_bf%d" % halves, bufs=5 - 2 * halves + (halves == 1), align_bytes=64)
             interleave(w_bf[:], w_raw[e][:, :, 0:n])
             home = W_HOME[e]
             codes = after_gate(home, [P, n], U32, 4 * n, "w_codes%d" % e)
@@ -177,22 +172,18 @@ def tile_moe_bds_lin_none_kernel(tc, dyT, w, gate, offs, pos1, pos2, pos3, pos4,
             interleave(late_bf[:, PACK * P * e : PACK * P * (e + 1)], w_raw[e][:, :, P:K])
 
         def quantize_late(i):
+            late_scales = arena.tile([P, E * P], U8, name="late_scales", offset=LAST_STAGE, align_bytes=64)
             nc.vector.quantize_mx(out=late_codes[:].bitcast(E4M3), scales=late_scales[:], in_=late_bf)
             for e in range(E):
                 w_codes[e, 1] = late_codes[:, e * P : (e + 1) * P]
                 w_scales[e, 1] = late_scales[:, e * P : (e + 1) * P]
 
-        def interleave_dy(i):
-            t0, t1 = DY_CUTS[i], DY_CUTS[i + 1]
-            r = t0 // BANK
-            interleave(dy_bf[r][:, PACK * (t0 - r * BANK) : PACK * (t1 - r * BANK)], dy_planes[r][:, :, t0 - r * BANK : t1 - r * BANK])
+        def interleave_dy(r):
+            interleave(dy_bf[r], dy_planes[r])
 
         def quantize_dy(r):
-            nc.vector.quantize_mx(
-                out=dy_codes[r][:].bitcast(E5M2),
-                scales=dy_scales[r][:],
-                in_=dy_bf[r],
-            )
+            dy_scales[r] = after_gate(E - 1, [P, BANK], U8, BANK, "dy_scales%d" % r)
+            nc.vector.quantize_mx(out=dy_codes[r][:].bitcast(E5M2), scales=dy_scales[r][:], in_=dy_bf[r])
 
         def product(dst, sums, e, h, codes, scales):
             nc.tensor.matmul_mx(
@@ -207,7 +198,7 @@ def tile_moe_bds_lin_none_kernel(tc, dyT, w, gate, offs, pos1, pos2, pos3, pos4,
             nc.scalar.copy(out=dst, in_=sums[:])
 
         second_banks = turned_banks + back_banks + [banks[3], banks[2], banks[0], banks[1]]
-        shared_banks = [banks[3], banks[3], banks[2], banks[0]]
+        shared_banks = [banks[3], banks[2], banks[0], banks[1]]
 
         def first_half(e):
             product(dx[0][:, e * C : (e + 1) * C], banks[e % 3], e, 0, g_codes[e], g_scales[e])
@@ -247,20 +238,11 @@ def tile_moe_bds_lin_none_kernel(tc, dyT, w, gate, offs, pos1, pos2, pos3, pos4,
         for step in ORDER.split():
             steps[step[0]](int(step[1]))
 
-        def quarters(tile, first, count):
-            return [tile[:, q * BANK : (q + 1) * BANK] for q in range(first, first + count)]
-
-        spare = [after_gate(e, [P, TOP * BANK], F32, GATE_BYTES, "spare%d" % e) for e in range(2)]
-        fetch_rooms = [
-            quarters(late_stage, 2, 2) + quarters(first_stage, 0, 2),
-            quarters(late_stage, 0, 2) + quarters(dy_raw[1], 0, 2),
-            quarters(spare[0], 0, TOP),
-            quarters(spare[1], 0, TOP),
+        spare = [after_gate(e, [P, 2 * T], F32, GATE_BYTES, "spare%d" % e) for e in range(2)]
+        fetched = [
+            [late_stage[:, T : 2 * T], first_stage[:], late_stage[:, 0:T], dy_raw[1][:, 0:T]],
+            [spare[i // 2][:, (i % 2) * T : (i % 2 + 1) * T] for i in range(TOP)],
         ]
-
-        def fetch(dst, h, r, i):
-            cols = BANK // STRIPE
-            nc.vector.tensor_copy(dst[i], dx[h][:].indirect(token_slots[i][:, r * cols : (r + 1) * cols]))
 
         def turn(dst, src, first, last):
             blocks = BANK // P
@@ -274,40 +256,35 @@ def tile_moe_bds_lin_none_kernel(tc, dyT, w, gate, offs, pos1, pos2, pos3, pos4,
                     is_transpose=True,
                 )
 
-        def summed(h, r, fetched, terms):
-            turned = turned_banks[(h * RANGES + r) % TB]
-            turn(turned, ds[h, r], True, False)
-            for i in range(terms):
-                turn(turned, fetched[i], False, i == terms - 1)
-            turned_sb = ring.tile([P, BANK], F32, name="turned_sb", tag="w_raw", bufs=E)
-            nc.scalar.copy(out=turned_sb[:], in_=turned[:])
-            back = back_banks[(h * RANGES + r) % TB]
-            for b in range(BANK // P):
-                nc.tensor.transpose(back[:, b * P : (b + 1) * P], turned_sb[:, b * P : (b + 1) * P], ident[:])
-            return back
-
-        def store(h, r, result):
-            nc.sync.dma_start(out[h * P : (h + 1) * P, r * BANK : (r + 1) * BANK], result[:])
-
-        for r in range(RANGES):
-            fetched = fetch_rooms[r]
+        def summed(h, terms):
+            for r in range(RANGES):
+                turn(turned_banks[r], ds[h, r], True, False)
             for i in range(TOP):
-                fetch(fetched, 0, r, i)
-            back = summed(0, r, fetched, TOP)
-            result = ring.tile([P, BANK], F32, name="result", tag="w_raw", bufs=E)
-            nc.scalar.copy(out=result[:], in_=back[:])
-            store(0, r, result)
+                cuts = RANGES if h == 1 and i >= TOP - 2 else 1
+                for c in range(cuts):
+                    t0, t1 = c * T // cuts, (c + 1) * T // cuts
+                    offsets = token_slots[i][:, t0 // STRIPE : t1 // STRIPE]
+                    nc.vector.tensor_copy(fetched[h][i][:, t0:t1], dx[h][:].indirect(offsets))
+                if i < terms:
+                    for r in range(RANGES):
+                        turn(turned_banks[r], fetched[h][i][:, r * BANK : (r + 1) * BANK], False, i == terms - 1)
+            for r in range(RANGES):
+                turned_sb = ring.tile([P, BANK], F32, name="turned_sb", tag="w_raw", bufs=E)
+                nc.scalar.copy(out=turned_sb[:], in_=turned_banks[r][:])
+                for b in range(BANK // P):
+                    nc.tensor.transpose(back_banks[r][:, b * P : (b + 1) * P], turned_sb[:, b * P : (b + 1) * P], ident[:])
 
-        tail = []
+        summed(0, TOP)
         for r in range(RANGES):
-            fetched = fetch_rooms[RANGES + r]
-            for i in range(TOP - 1):
-                fetch(fetched, 1, r, i)
-            tail.append((fetched, summed(1, r, fetched, TOP - 1)))
-        for r in range(RANGES):
-            fetch(tail[r][0], 1, r, TOP - 1)
-        for r in range(RANGES):
-            fetched, back = tail[r]
             result = ring.tile([P, BANK], F32, name="result", tag="w_raw", bufs=E)
-            nc.vector.tensor_tensor(result[:], fetched[TOP - 1], back[:], ADD)
-            store(1, r, result)
+            nc.scalar.copy(out=result[:], in_=back_banks[r][:])
+            nc.sync.dma_start(out[0:P, r * BANK : (r + 1) * BANK], result[:])
+
+        summed(1, TOP - 1)
+        for t0, t1 in ((0, 512), (512, 768), (768, 1024)):
+            r = t0 // BANK
+            result = ring.tile([P, t1 - t0], F32, name="result", tag="w_raw", bufs=E)
+            nc.vector.tensor_tensor(
+                result[:], fetched[1][TOP - 1][:, t0:t1], back_banks[r][:, t0 - r * BANK : t1 - r * BANK], ADD
+            )
+            nc.sync.dma_start(out[P : 2 * P, t0:t1], result[:])

from contextlib import ExitStack

import concourse.mybir as mybir
from concourse.masks import make_identity

K, T, E, C, N = 256, 1024, 8, 512, 512
TOP = 4
FLOPS = 2 * N * K * (E * C + T)

F32 = mybir.dt.float32
BF16 = mybir.dt.bfloat16
U32 = mybir.dt.uint32
U16 = mybir.dt.uint16
U8 = mybir.dt.uint8
E4M3 = mybir.dt.float8_e4m3fn_x4
E5M2 = mybir.dt.float8_e5m2_x4
MULT = mybir.AluOpType.mult
ADD = mybir.AluOpType.add

P = 128
PACK = 4
STRIPE = 16
BANK = 512
HALVES = K // P
RANGES = T // BANK
LAST_PIECES = (256, 128, 128)
GATE_BYTES = 4 * PACK * C
LAST_STAGE = E * GATE_BYTES + 4096
W_HOME = (3, 3, 3, 4, 5, 6, 7, 7, 7)
TB = 2
LOADS = "p2 w0 w1 g3 w2 w3 w4 g4 w8 w5 g5 d0 w6 g6 w7 g7 l0 d1"
ORDER = "G2 I0 I1 G3 A0 A1 I2 A2 G4 I3 A3 E0 E1 E2 G5 I4 A4 E3 G6 I5 A5 E4 G7 I6 A6 A7 D0 B0 B1 B2 B3 B4 B5 B6 B7 I7 E5 E6 E7 Q0 W8 H0 D1 Q1 F0 F1 F2 F3 F4 F5 F6 F7 S0 S1 S2 S3"


def tile_moe_bds_lin_none_kernel(tc, dyT, w, gate, offs, pos1, pos2, pos3, pos4, out):
    nc = tc.nc
    with ExitStack() as ctx:
        keep = ctx.enter_context(tc.tile_pool(name="keep", bufs=1))
        ring = ctx.enter_context(tc.tile_pool(name="ring", bufs=2))
        arena = ctx.enter_context(tc.tile_pool(name="arena", bufs=1))
        psum = ctx.enter_context(tc.psum_pool(name="psum", bufs=2))

        dy_rows = dyT.rearrange("(p j) t -> p j t", j=PACK)
        gate_rows = gate.rearrange("(p j) s -> p j s", j=PACK)

        def interleave(dst, src):
            nc.scalar.copy(
                dst.rearrange("p (c i j) -> p c j i", i=4, j=PACK),
                src.rearrange("p j (c i) -> p c j i", i=4),
            )

        slot_token = keep.tile([P, E * C // STRIPE], U16, name="slot_token")
        nc.sync.dma_start(slot_token[:], offs)

        planes = [keep.tile([P, T], F32, name="plane%d" % j) for j in range(PACK)]
        gates = {}
        w_raw = {}

        def new_gate(e):
            head = arena.tile([P, PACK - 1, C], F32, name="gate%d" % e, offset=e * GATE_BYTES, align_bytes=64)
            last = arena.tile([P, C], F32, name="gate_last%d" % e, offset=(e + 1) * GATE_BYTES - 4 * C, align_bytes=64)
            gates[e] = [head[:, j, :] for j in range(PACK - 1)] + [last[:]]
            return head

        def load_gate(e):
            head = new_gate(e)
            nc.sync.dma_start(head[:], gate_rows[:, 0 : PACK - 1, e * C : (e + 1) * C])
            nc.sync.dma_start(gates[e][PACK - 1], gate_rows[:, PACK - 1, e * C : (e + 1) * C])

        def load_gate_planes(e):
            new_gate(e)
            for j in range(PACK):
                nc.sync.dma_start(gates[e][j], gate_rows[:, j, e * C : (e + 1) * C])

        def load_w(e):
            w_raw[e] = ring.tile([P, PACK, K], F32, name="w_raw%d" % e, tag="w_raw", bufs=E)
            nc.sync.dma_start(w_raw[e][:], w[e].rearrange("(p j) k -> p j k", j=PACK))

        new_gate(0)
        new_gate(1)
        for j in range(PACK):
            nc.sync.dma_start(planes[j][:], dy_rows[:, j, :])
            for e in range(2):
                nc.sync.dma_start(gates[e][j], gate_rows[:, j, e * C : (e + 1) * C])

        ident = keep.tile([P, P], F32, name="ident")
        make_identity(nc, ident[:])

        dx = [keep.tile([P, E * C], F32, name="dx%d" % h) for h in range(HALVES)]
        g_codes, g_scales = {}, {}
        used = {e: 0 for e in range(E + 1)}

        def after_gate(e, shape, dtype, size, name):
            start = e * GATE_BYTES + used[e]
            used[e] += size
            assert used[e] <= GATE_BYTES
            return arena.tile(shape, dtype, name=name, offset=start, align_bytes=64)

        w_codes, w_scales = {}, {}
        late_codes = keep.tile([P, E * P], U32, name="late_codes", align_bytes=64)
        late_stage = keep.tile([P, TOP * BANK], F32, name="late_stage", align_bytes=64)
        late_bf = late_stage[:].bitcast(BF16)
        dy_codes = [keep.tile([P, BANK], U32, name="dy_codes%d" % r, align_bytes=64) for r in range(RANGES)]
        dy_scales = {}
        dy_raw = [keep.tile([P, PACK * BANK], F32, name="dy_raw%d" % r) for r in range(RANGES)]
        dy_planes = [raw[:].rearrange("p (j t) -> p j t", j=PACK) for raw in dy_raw]
        first_stage = keep.tile([P, T], F32, name="first_stage", align_bytes=64)
        dy_bf = [first_stage[:].bitcast(BF16), late_bf[:, 0 : PACK * BANK]]
        token_slots = [keep.tile([P, T // STRIPE], U16, name="token_slots%d" % r) for r in range(TOP)]
        banks = [psum.tile([P, BANK], F32, name="bank%d" % b, bufs=1) for b in range(4)]
        turned_banks = [psum.tile([P, BANK], F32, name="turned%d" % b, bufs=1) for b in range(TB)]
        back_banks = [psum.tile([P, BANK], F32, name="back%d" % b, bufs=1) for b in range(TB)]
        ds = {}
        g = {0: keep.tile([P, PACK * C], F32, name="g_first")}

        def load_dy(r):
            nc.sync.dma_start(dy_planes[r], dy_rows[:, :, r * BANK : (r + 1) * BANK])

        def load_lists(i):
            for r, pos in enumerate((pos1, pos2, pos3, pos4)):
                nc.sync.dma_start(token_slots[r][:], pos)

        def piece(e, c0, n):
            return g[e][:, PACK * c0 : PACK * (c0 + n)].rearrange("p (j c) -> p j c", j=PACK)

        def gather_plane(e, j, c0, n):
            s0 = e * C + c0
            nc.vector.tensor_tensor(
                piece(e, c0, n)[:, j, :],
                planes[j][:].indirect(slot_token[:, s0 // STRIPE : (s0 + n) // STRIPE]),
                gates[e][j][:, c0 : c0 + n],
                MULT,
            )

        def pieces(e):
            sizes = LAST_PIECES if e == E - 1 else (C,)
            return [(sum(sizes[:i]), n) for i, n in enumerate(sizes)]

        def gather_expert(e):
            g[e] = ring.tile([P, PACK * C], F32, name="g")
            for c0, n in pieces(e):
                for j in range(PACK):
                    gather_plane(e, j, c0, n)

        def quantize_g(e):
            home = max(e + 1, 2)
            g_codes[e] = after_gate(home, [P, C], U32, 4 * C, "g_codes%d" % e)
            g_scales[e] = after_gate(home, [P, C], U8, C, "g_scales%d" % e)
            for c0, n in pieces(e):
                if e == E - 1 and c0 + n == C:
                    g_bf = arena.tile([P, PACK * n], BF16, name="last_bf", offset=LAST_STAGE, align_bytes=64)
                else:
                    g_bf = ring.tile([P, PACK * n], BF16, name="g_bf", bufs=3, align_bytes=64)
                interleave(g_bf[:], piece(e, c0, n))
                nc.vector.quantize_mx(
                    out=g_codes[e][:, c0 : c0 + n].bitcast(E5M2), scales=g_scales[e][:, c0 : c0 + n], in_=g_bf[:]
                )

        def quantize_w(e, halves):
            n = halves * P
            w_bf = ring.tile([P, PACK * n], BF16, name="w_bf%d" % halves, bufs=5 - 2 * halves + (halves == 1), align_bytes=64)
            interleave(w_bf[:], w_raw[e][:, :, 0:n])
            home = W_HOME[e]
            codes = after_gate(home, [P, n], U32, 4 * n, "w_codes%d" % e)
            scales = after_gate(home, [P, n], U8, n, "w_scales%d" % e)
            nc.vector.quantize_mx(out=codes[:].bitcast(E4M3), scales=scales[:], in_=w_bf[:])
            for h in range(halves):
                w_codes[e, h] = codes[:, h * P : (h + 1) * P]
                w_scales[e, h] = scales[:, h * P : (h + 1) * P]

        def interleave_late(e):
            interleave(late_bf[:, PACK * P * e : PACK * P * (e + 1)], w_raw[e][:, :, P:K])

        def quantize_late(i):
            late_scales = arena.tile([P, E * P], U8, name="late_scales", offset=LAST_STAGE, align_bytes=64)
            nc.vector.quantize_mx(out=late_codes[:].bitcast(E4M3), scales=late_scales[:], in_=late_bf)
            for e in range(E):
                w_codes[e, 1] = late_codes[:, e * P : (e + 1) * P]
                w_scales[e, 1] = late_scales[:, e * P : (e + 1) * P]

        def interleave_dy(r):
            interleave(dy_bf[r], dy_planes[r])

        def quantize_dy(r):
            dy_scales[r] = after_gate(E - 1, [P, BANK], U8, BANK, "dy_scales%d" % r)
            nc.vector.quantize_mx(out=dy_codes[r][:].bitcast(E5M2), scales=dy_scales[r][:], in_=dy_bf[r])

        def product(dst, sums, e, h, codes, scales):
            nc.tensor.matmul_mx(
                out=sums[:],
                lhsT=w_codes[e, h].bitcast(E4M3),
                lhsT_scale=w_scales[e, h],
                rhs=codes[:].bitcast(E5M2),
                rhs_scale=scales[:],
                start=True,
                stop=True,
            )
            nc.scalar.copy(out=dst, in_=sums[:])

        second_banks = turned_banks + back_banks + [banks[3], banks[2], banks[0], banks[1]]
        shared_banks = [banks[3], banks[2], banks[0], banks[1]]

        def first_half(e):
            product(dx[0][:, e * C : (e + 1) * C], banks[e % 3], e, 0, g_codes[e], g_scales[e])

        def second_half(e):
            product(dx[1][:, e * C : (e + 1) * C], second_banks[e], e, 1, g_codes[e], g_scales[e])

        def shared(i):
            h, r = divmod(i, RANGES)
            ds[h, r] = ring.tile([P, BANK], F32, name="ds", tag="w_raw", bufs=E)
            product(ds[h, r][:], shared_banks[i], E, h, dy_codes[r], dy_scales[r])

        steps = {
            "g": load_gate,
            "p": load_gate_planes,
            "w": load_w,
            "d": load_dy,
            "l": load_lists,
            "G": gather_expert,
            "I": quantize_g,
            "W": lambda e: quantize_w(e, HALVES),
            "A": lambda e: quantize_w(e, 1),
            "B": interleave_late,
            "H": quantize_late,
            "D": interleave_dy,
            "Q": quantize_dy,
            "E": first_half,
            "F": second_half,
            "S": shared,
        }
        for step in LOADS.split():
            steps[step[0]](int(step[1]))
        g[1] = ring.tile([P, PACK * C], F32, name="g")
        for j in range(PACK):
            for e in range(2):
                gather_plane(e, j, 0, C)
        for step in ORDER.split():
            steps[step[0]](int(step[1]))

        spare = [after_gate(e, [P, 2 * T], F32, GATE_BYTES, "spare%d" % e) for e in range(2)]
        fetched = [
            [late_stage[:, T : 2 * T], first_stage[:], late_stage[:, 0:T], dy_raw[1][:, 0:T]],
            [spare[i // 2][:, (i % 2) * T : (i % 2 + 1) * T] for i in range(TOP)],
        ]

        def turn(dst, src, first, last):
            blocks = BANK // P
            for b in range(blocks):
                nc.tensor.matmul(
                    dst[:, b * P : (b + 1) * P],
                    src[:, b * P : (b + 1) * P],
                    ident[:],
                    start=(first and b == 0),
                    stop=(last and b == blocks - 1),
                    is_transpose=True,
                )

        def summed(h, terms):
            for r in range(RANGES):
                turn(turned_banks[r], ds[h, r], True, False)
            for i in range(TOP):
                cuts = RANGES if h == 1 and i >= TOP - 2 else 1
                for c in range(cuts):
                    t0, t1 = c * T // cuts, (c + 1) * T // cuts
                    offsets = token_slots[i][:, t0 // STRIPE : t1 // STRIPE]
                    nc.vector.tensor_copy(fetched[h][i][:, t0:t1], dx[h][:].indirect(offsets))
                if i < terms:
                    for r in range(RANGES):
                        turn(turned_banks[r], fetched[h][i][:, r * BANK : (r + 1) * BANK], False, i == terms - 1)
            for r in range(RANGES):
                turned_sb = ring.tile([P, BANK], F32, name="turned_sb", tag="w_raw", bufs=E)
                nc.scalar.copy(out=turned_sb[:], in_=turned_banks[r][:])
                for b in range(BANK // P):
                    nc.tensor.transpose(back_banks[r][:, b * P : (b + 1) * P], turned_sb[:, b * P : (b + 1) * P], ident[:])

        summed(0, TOP)
        for r in range(RANGES):
            result = ring.tile([P, BANK], F32, name="result", tag="w_raw", bufs=E)
            nc.scalar.copy(out=result[:], in_=back_banks[r][:])
            nc.sync.dma_start(out[0:P, r * BANK : (r + 1) * BANK], result[:])

        summed(1, TOP - 1)
        for t0, t1 in ((0, 512), (512, 768), (768, 1024)):
            r = t0 // BANK
            result = ring.tile([P, t1 - t0], F32, name="result", tag="w_raw", bufs=E)
            nc.vector.tensor_tensor(
                result[:], fetched[1][TOP - 1][:, t0:t1], back_banks[r][:, t0 - r * BANK : t1 - r * BANK], ADD
            )
            nc.sync.dma_start(out[P : 2 * P, t0:t1], result[:])
